import numpy as np, ml_dtypes
CORES = [78,86,94,102,110,118]
N = 6
F = 256
GROUPS = [[0,3],[1,4],[2,5]]
def setup_inputs(rng):
    return {"x": rng.standard_normal((N, 128, F), dtype=np.float32).astype(ml_dtypes.bfloat16), "w": (rng.standard_normal((N, 128, 128), dtype=np.float32) / 11).astype(ml_dtypes.bfloat16)}
def setup_inputs_big(rng):
    d = setup_inputs(rng)
    for k in ("x", "w"): d[k] = (d[k].astype(np.float32) * 1024.0).astype(d[k].dtype)
    return d
def setup_inputs_small(rng):
    d = setup_inputs(rng)
    for k in ("x", "w"): d[k] = (d[k].astype(np.float32) * (1 / 1024.0)).astype(d[k].dtype)
    return d
def setup_inputs_apart(rng):
    d = setup_inputs(rng)
    f = (10.0 ** rng.permutation(np.linspace(-1.5, 1.5, N))).astype(np.float32).reshape(N, 1, 1)
    for k in ("x", "w"): d[k] = (d[k].astype(np.float32) * f).astype(d[k].dtype)
    return d
def reference(x, w):
    X, W = x.astype(np.float64), w.astype(np.float64)
    s = sum(W[g[0]].T @ np.maximum(sum(X[j] for j in g), 0.0) for g in GROUPS).astype(ml_dtypes.bfloat16)
    return {"y": np.broadcast_to(s, (N,) + s.shape)}

@@ -1,0 +1,121 @@
+from concourse.bass import DstId, RemoteDMATransfer
+from concourse.mybir import AluOpType
+
+F = 256
+K = 128
+
+SCRATCH = {
+    "xw": ("sbuf", [128, F + K], "bfloat16"),
+    "pw": ("sbuf", [128, F + K], "bfloat16"),
+    "zero": ("sbuf", [128, F], "bfloat16"),
+    "t": ("sbuf", [128, F], "bfloat16"),
+    "p": ("sbuf", [128, F], "bfloat16"),
+    "land0": ("sbuf", [128, F], "bfloat16"),
+    "land1": ("sbuf", [128, F], "bfloat16"),
+    "land2": ("sbuf", [128, F], "bfloat16"),
+    "ysb": ("sbuf", [128, F], "bfloat16"),
+    "xf": ("psum", [128, 512], "float32"),
+    "sf": ("psum", [128, 512], "float32"),
+    "pf": ("psum", [128, 512], "float32"),
+    "af": ("psum", [128, 512], "float32"),
+}
+SEMAPHORES = ["ldx", "ldw", "xarr", "sent", "zs", "cs", "ss", "ts", "ms", "ps", "as1", "ys", "st",
+              "arr0", "arr1", "arr2"]
+
+
+def _engines(mask):
+    return bin(mask).count("1")
+
+
+def rank_program(g, core, T, topo):
+    rank = T.rank_of(core)
+    if rank is None:
+        return
+    groups = T.tables["GROUPS"]
+    cores = T.cores
+    n = len(cores)
+    sem = T.sem
+    gi = [k for k, m in enumerate(groups) if rank in m][0]
+    members = groups[gi]
+    lead = members[0] == rank
+    partner = [m for m in members if m != rank][0]
+
+    def sender_of(k, d):
+        for near in (topo.same_plane, topo.mates):
+            for m in groups[k]:
+                if near(topo.chip(cores[m]), topo.chip(cores[d])) and topo.may_write(cores[m], cores[d]):
+                    return m
+        return [m for m in groups[k] if topo.may_write(cores[m], cores[d])][0]
+
+    dests = sorted([d for d in range(n) if d not in members and sender_of(gi, d) == rank],
+                   key=lambda d: (d - rank) % n)
+    sources = sorted([(sender_of(k, rank), k) for k in range(len(groups)) if k != gi],
+                     key=lambda s: (rank - s[0]) % n)
+
+    v, pe = g.vector, g.tensor
+
+    g.sync.dma_start(T.xw[:, 0:F], T.x[:]).then_inc(sem.ldx, 16)
+    if lead:
+        g.scalar.dma_start(T.xw[:, F:F + K], T.w[:]).then_inc(sem.ldw, 16)
+
+    width = F + K if lead else F
+    rid, pid, _ = topo.addr(cores[partner])
+    m1 = topo.mask(core, cores[partner])
+    g.wait_ge(sem.ldx, 16)
+    if lead:
+        g.wait_ge(sem.ldw, 16)
+    g.remote_dma(out_ap=T.pw[:, 0:width], in_ap=T.xw[:, 0:width], remote_sem=sem.xarr, local_sem=sem.sent,
+                 pid=pid, routing_id=rid, dma_engine_mask=m1)
+    n_in = _engines(topo.mask(cores[partner], core))
+
+    v.memset(T.zero[:], 0.0).then_inc(sem.zs, 1)
+    v.wait_ge(sem.ldx, 16)
+    v.tensor_copy(T.xf[:, 0:F], T.xw[:, 0:F]).then_inc(sem.cs, 1)
+    v.wait_ge(sem.zs, 1)
+    v.wait_ge(sem.cs, 1)
+
+    v.wait_ge(sem.xarr, n_in)
+    v.tensor_tensor(T.sf[:, 0:F], T.xf[:, 0:F], T.pw[:, 0:F], AluOpType.add).then_inc(sem.ss, 1)
+    v.wait_ge(sem.ss, 1)
+    v.tensor_tensor(T.t[:], T.sf[:, 0:F], T.zero[:], AluOpType.max).then_inc(sem.ts, 1)
+
+    if lead:
+        pe.wait_ge(sem.ldw, 16)
+        wmat = T.xw[:, F:F + K]
+    else:
+        pe.wait_ge(sem.xarr, n_in)
+        wmat = T.pw[:, F:F + K]
+    pe.wait_ge(sem.ts, 1)
+    pe.matmul(T.pf[:, 0:F], wmat, T.t[:], start=True, stop=True).then_inc(sem.ms, 1)
+    v.wait_ge(sem.ms, 1)
+    v.tensor_copy(T.p[:], T.pf[:, 0:F]).then_inc(sem.ps, 1)
+
+    m2 = 0
+    if dests:
+        m2 = topo.mask(core, cores[dests[0]])
+        for d in dests:
+            m2 &= topo.mask(core, cores[d])
+        ids = []
+        for d in dests:
+            r, q, _ = topo.addr(cores[d])
+            ids.append(DstId(rid=r, pnc=q))
+        g.wait_ge(sem.ps, 1)
+        g.remote_dma_fused([RemoteDMATransfer(dst_ids=ids, dma_engine_mask=m2, remote_sem=sem["arr%d" % gi],
+                                              srcs=[T.p[:]], dsts=[T["land%d" % gi][:] for _ in dests], alu_op=0)],
+                           local_sem=sem.sent)
+
+    acc = T.pf
+    for i, (s, k) in enumerate(sources):
+        cnt = _engines(topo.mask(cores[s], core))
+        v.wait_ge(sem["arr%d" % k], cnt)
+        if i + 1 < len(sources):
+            v.tensor_tensor(T.af[:, 0:F], acc[:, 0:F], T["land%d" % k][:], AluOpType.add).then_inc(sem.as1, 1)
+            v.wait_ge(sem.as1, 1)
+            acc = T.af
+        else:
+            v.tensor_tensor(T.ysb[:], acc[:, 0:F], T["land%d" % k][:], AluOpType.add).then_inc(sem.ys, 1)
+    g.sync.wait_ge(sem.ys, 1)
+    g.sync.dma_start(T.y[:], T.ysb[:]).then_inc(sem.st, 16)
+    g.sync.wait_ge(sem.st, 16)
+
+    g.wait_ge(sem.sent, _engines(m1) + _engines(m2))

@@ -3,24 +3,26 @@ from concourse.mybir import AluOpType
 
 F = 256
 K = 128
+NH = 2
+H = F // NH
 
 SCRATCH = {
     "xw": ("sbuf", [128, F + K], "bfloat16"),
     "pw": ("sbuf", [128, F + K], "bfloat16"),
     "zero": ("sbuf", [128, F], "bfloat16"),
-    "t": ("sbuf", [128, F], "bfloat16"),
+    "m": ("sbuf", [128, F], "bfloat16"),
     "p": ("sbuf", [128, F], "bfloat16"),
     "land0": ("sbuf", [128, F], "bfloat16"),
     "land1": ("sbuf", [128, F], "bfloat16"),
     "land2": ("sbuf", [128, F], "bfloat16"),
     "ysb": ("sbuf", [128, F], "bfloat16"),
-    "xf": ("psum", [128, 512], "float32"),
-    "sf": ("psum", [128, 512], "float32"),
-    "pf": ("psum", [128, 512], "float32"),
-    "af": ("psum", [128, 512], "float32"),
+    "nx": ("psum", [128, 512], "float32"),
+    "af": ("psum", [128, 2 * F], "float32"),
 }
-SEMAPHORES = ["ldx", "ldw", "xarr", "sent", "zs", "cs", "ss", "ts", "ms", "ps", "as1", "ys", "st",
-              "arr0", "arr1", "arr2"]
+for _c in range(NH):
+    SCRATCH["pf%d" % _c] = ("psum", [128, 512], "float32")
+SEMAPHORES = (["ldx", "ldw", "xarr", "sent", "zs", "ns", "ps", "gs", "as1", "ys", "st", "arr0", "arr1", "arr2"]
+              + ["%s%d" % (s, c) for s in ("ts", "ms") for c in range(NH)])
 
 
 def _engines(mask):
@@ -51,6 +53,7 @@ def rank_program(g, core, T, topo):
                    key=lambda d: (d - rank) % n)
     sources = sorted([(sender_of(k, rank), k) for k in range(len(groups)) if k != gi],
                      key=lambda s: (rank - s[0]) % n)
+    blocks = [(c * H, (c + 1) * H) for c in range(NH)]
 
     v, pe = g.vector, g.tensor
 
@@ -69,51 +72,52 @@ def rank_program(g, core, T, topo):
     n_in = _engines(topo.mask(cores[partner], core))
 
     v.memset(T.zero[:], 0.0).then_inc(sem.zs, 1)
-    v.wait_ge(sem.ldx, 16)
-    v.tensor_copy(T.xf[:, 0:F], T.xw[:, 0:F]).then_inc(sem.cs, 1)
     v.wait_ge(sem.zs, 1)
-    v.wait_ge(sem.cs, 1)
+    v.wait_ge(sem.ldx, 16)
+    v.tensor_tensor(T.nx[:, 0:F], T.zero[:], T.xw[:, 0:F], AluOpType.subtract).then_inc(sem.ns, 1)
+    v.wait_ge(sem.ns, 1)
 
-    v.wait_ge(sem.xarr, n_in)
-    v.tensor_tensor(T.sf[:, 0:F], T.xf[:, 0:F], T.pw[:, 0:F], AluOpType.add).then_inc(sem.ss, 1)
-    v.wait_ge(sem.ss, 1)
-    v.tensor_tensor(T.t[:], T.sf[:, 0:F], T.zero[:], AluOpType.max).then_inc(sem.ts, 1)
-
+    pe.wait_ge(sem.ldx, 16)
     if lead:
         pe.wait_ge(sem.ldw, 16)
         wmat = T.xw[:, F:F + K]
     else:
         pe.wait_ge(sem.xarr, n_in)
         wmat = T.pw[:, F:F + K]
-    pe.wait_ge(sem.ts, 1)
-    pe.matmul(T.pf[:, 0:F], wmat, T.t[:], start=True, stop=True).then_inc(sem.ms, 1)
-    v.wait_ge(sem.ms, 1)
-    v.tensor_copy(T.p[:], T.pf[:, 0:F]).then_inc(sem.ps, 1)
+    for c, (lo, hi) in enumerate(blocks):
+        pe.matmul(T["pf%d" % c][:, 0:H], wmat, T.xw[:, lo:hi], start=True, stop=False)
 
-    m2 = 0
-    if dests:
-        m2 = topo.mask(core, cores[dests[0]])
-        for d in dests:
-            m2 &= topo.mask(core, cores[d])
-        ids = []
-        for d in dests:
-            r, q, _ = topo.addr(cores[d])
-            ids.append(DstId(rid=r, pnc=q))
-        g.wait_ge(sem.ps, 1)
-        g.remote_dma_fused([RemoteDMATransfer(dst_ids=ids, dma_engine_mask=m2, remote_sem=sem["arr%d" % gi],
-                                              srcs=[T.p[:]], dsts=[T["land%d" % gi][:] for _ in dests], alu_op=0)],
-                           local_sem=sem.sent)
+    v.wait_ge(sem.xarr, n_in)
+    for c, (lo, hi) in enumerate(blocks):
+        v.tensor_tensor(T.m[:, lo:hi], T.nx[:, lo:hi], T.pw[:, lo:hi], AluOpType.max).then_inc(sem["ts%d" % c], 1)
+    for c, (lo, hi) in enumerate(blocks):
+        pe.wait_ge(sem["ts%d" % c], 1)
+        pe.matmul(T["pf%d" % c][:, 0:H], wmat, T.m[:, lo:hi], start=False, stop=True).then_inc(sem["ms%d" % c], 1)
+    for c, (lo, hi) in enumerate(blocks):
+        v.wait_ge(sem["ms%d" % c], 1)
+        v.tensor_copy(T.p[:, lo:hi], T["pf%d" % c][:, 0:H]).then_inc(sem.ps, 1)
 
-    acc = T.pf
-    for i, (s, k) in enumerate(sources):
-        cnt = _engines(topo.mask(cores[s], core))
-        v.wait_ge(sem["arr%d" % k], cnt)
-        if i + 1 < len(sources):
-            v.tensor_tensor(T.af[:, 0:F], acc[:, 0:F], T["land%d" % k][:], AluOpType.add).then_inc(sem.as1, 1)
-            v.wait_ge(sem.as1, 1)
-            acc = T.af
-        else:
-            v.tensor_tensor(T.ysb[:], acc[:, 0:F], T["land%d" % k][:], AluOpType.add).then_inc(sem.ys, 1)
+    m2 = topo.mask(core, cores[dests[0]])
+    ids = []
+    for d in dests:
+        m2 &= topo.mask(core, cores[d])
+        r, q, _ = topo.addr(cores[d])
+        ids.append(DstId(rid=r, pnc=q))
+    g.wait_ge(sem.ps, NH)
+    g.remote_dma_fused([RemoteDMATransfer(dst_ids=ids, dma_engine_mask=m2, remote_sem=sem["arr%d" % gi],
+                                          srcs=[T.p[:]], dsts=[T["land%d" % gi][:] for _ in dests], alu_op=0)],
+                       local_sem=sem.sent)
+
+    for c, (lo, hi) in enumerate(blocks):
+        v.tensor_copy(T.af[:, lo:hi], T["pf%d" % c][:, 0:H]).then_inc(sem.gs, 1)
+    v.wait_ge(sem.gs, NH)
+
+    (s1, k1), (s2, k2) = sources
+    v.wait_ge(sem["arr%d" % k1], _engines(topo.mask(cores[s1], core)))
+    v.tensor_tensor(T.af[:, F:2 * F], T.af[:, 0:F], T["land%d" % k1][:], AluOpType.add).then_inc(sem.as1, 1)
+    v.wait_ge(sem.as1, 1)
+    v.wait_ge(sem["arr%d" % k2], _engines(topo.mask(cores[s2], core)))
+    v.tensor_tensor(T.ysb[:], T.af[:, F:2 * F], T["land%d" % k2][:], AluOpType.add).then_inc(sem.ys, 1)
     g.sync.wait_ge(sem.ys, 1)
     g.sync.dma_start(T.y[:], T.ysb[:]).then_inc(sem.st, 16)
     g.sync.wait_ge(sem.st, 16)

@@ -1,42 +1,104 @@
 from concourse.bass import DstId, RemoteDMATransfer
-from concourse.mybir import AluOpType
+from concourse.mybir import AluOpType, ActivationFunctionType
 
 F = 256
 K = 128
-NH = 2
-H = F // NH
+N0 = 112
+NB = 4
+B = F // NB
 
 SCRATCH = {
-    "xw": ("sbuf", [128, F + K], "bfloat16"),
-    "pw": ("sbuf", [128, F + K], "bfloat16"),
-    "zero": ("sbuf", [128, F], "bfloat16"),
-    "m": ("sbuf", [128, F], "bfloat16"),
-    "p": ("sbuf", [128, F], "bfloat16"),
-    "land0": ("sbuf", [128, F], "bfloat16"),
-    "land1": ("sbuf", [128, F], "bfloat16"),
-    "land2": ("sbuf", [128, F], "bfloat16"),
+    "xd": ("dram", [128, F], "bfloat16"),
+    "xs": ("sbuf", [128, F], "bfloat16"),
+    "xp": ("sbuf", [128, F], "bfloat16"),
+    "wd": ("dram", [128, K], "bfloat16"),
+    "wo": ("sbuf", [128, K], "bfloat16"),
+    "whd": ("dram", [128, K], "bfloat16"),
+    "ones": ("sbuf", [128, 128], "bfloat16"),
+    "ident": ("sbuf", [128, 128], "bfloat16"),
+    "s": ("sbuf", [128, F], "bfloat16"),
+    "t": ("sbuf", [128, F], "bfloat16"),
     "ysb": ("sbuf", [128, F], "bfloat16"),
-    "nx": ("psum", [128, 512], "float32"),
-    "af": ("psum", [128, 2 * F], "float32"),
+    "xf": ("psum", [128, 512], "float32"),
+    "sf": ("psum", [128, 512], "float32"),
 }
-for _c in range(NH):
-    SCRATCH["pf%d" % _c] = ("psum", [128, 512], "float32")
-SEMAPHORES = (["ldx", "ldw", "xarr", "sent", "zs", "ns", "ps", "gs", "as1", "ys", "st", "arr0", "arr1", "arr2"]
-              + ["%s%d" % (s, c) for s in ("ts", "ms") for c in range(NH)])
+for _k in range(3):
+    SCRATCH["wl%d" % _k] = ("sbuf", [128, K], "bfloat16")
+    SCRATCH["tl%d" % _k] = ("sbuf", [128, F], "bfloat16")
+for _c in range(NB):
+    SCRATCH["yf%d" % _c] = ("psum", [128, 512], "float32")
+SEMAPHORES = (["ldd", "ldx", "ldwd", "ldw", "xarr", "sent", "cs", "fill", "ids", "ps", "as0", "ts", "ys", "st",
+               "wharr"]
+              + ["%s%d" % (s, k) for s in ("warr", "arr") for k in range(3)]
+              + ["ms%d" % c for c in range(NB)])
 
 
 def _engines(mask):
     return bin(mask).count("1")
 
 
+def _every_other(mask):
+    bits = [i for i in range(mask.bit_length()) if (mask >> i) & 1]
+    return sum(1 << i for i in bits[::2])
+
+
+def _forwarders(T, topo, groups):
+    cores = T.cores
+    plan = {}
+    for k, members in enumerate(groups):
+        lead = cores[members[0]]
+        idle = [c for c in range(topo.CHIPS * topo.CORES_PER_CHIP)
+                if topo.chip(c) == topo.chip(lead) and topo.die(c) != topo.die(lead) and T.rank_of(c) is None]
+        others = [d for d in range(len(cores)) if d != members[0]]
+        near = [d for d in others if topo.same_plane(topo.chip(lead), topo.chip(cores[d]))]
+        far = [d for d in others if d not in near]
+        owners = [c for c in idle if all(topo.may_write(c, cores[d]) for d in far)]
+        rest = [c for c in idle if c not in owners and all(topo.may_write(c, cores[d]) for d in near)]
+        half = (len(far) + 1) // 2
+        plan[k] = [(owners[0], far[:half]), (owners[1], far[half:]), (rest[0], near)]
+    return plan
+
+
 def rank_program(g, core, T, topo):
-    rank = T.rank_of(core)
-    if rank is None:
-        return
     groups = T.tables["GROUPS"]
     cores = T.cores
     n = len(cores)
     sem = T.sem
+    plan = _forwarders(T, topo, groups)
+    rank = T.rank_of(core)
+
+    def w_mask(lead_core, helper):
+        off = [c for c in cores if topo.chip(c) != topo.chip(lead_core)][0]
+        m = topo.mask(lead_core, helper) & ~topo.mask(lead_core, off)
+        return _every_other(m if m else topo.mask(lead_core, helper))
+
+    def out_mask(src, served):
+        mk = topo.mask(src, cores[served[0]])
+        for d in served:
+            mk &= topo.mask(src, cores[d])
+        return mk
+
+    def ids_of(cs):
+        out = []
+        for c in cs:
+            r, q, _ = topo.addr(c)
+            out.append(DstId(rid=r, pnc=q))
+        return out
+
+    if rank is None:
+        for k in plan:
+            for h, served in plan[k]:
+                if h != core:
+                    continue
+                mk = out_mask(core, served)
+                g.wait_ge(sem.wharr, _engines(w_mask(cores[groups[k][0]], core)))
+                g.remote_dma_fused([RemoteDMATransfer(dst_ids=ids_of([cores[d] for d in served]), dma_engine_mask=mk,
+                                                      remote_sem=sem["warr%d" % k], srcs=[T.whd[:]],
+                                                      dsts=[T["wl%d" % k][:] for _ in served], alu_op=0)],
+                                   local_sem=sem.sent)
+                g.wait_ge(sem.sent, _engines(mk))
+        return
+
     gi = [k for k, m in enumerate(groups) if rank in m][0]
     members = groups[gi]
     lead = members[0] == rank
@@ -49,77 +111,96 @@ def rank_program(g, core, T, topo):
                     return m
         return [m for m in groups[k] if topo.may_write(cores[m], cores[d])][0]
 
+    def w_engines(k, d):
+        for h, served in plan[k]:
+            if d in served:
+                return _engines(out_mask(h, served))
+
     dests = sorted([d for d in range(n) if d not in members and sender_of(gi, d) == rank],
                    key=lambda d: (d - rank) % n)
     sources = sorted([(sender_of(k, rank), k) for k in range(len(groups)) if k != gi],
                      key=lambda s: (rank - s[0]) % n)
-    blocks = [(c * H, (c + 1) * H) for c in range(NH)]
+    blocks = [(c * B, (c + 1) * B) for c in range(NB)]
+    v, pe, sc = g.vector, g.tensor, g.scalar
+    relu, copy = ActivationFunctionType.Relu, ActivationFunctionType.Copy
 
-    v, pe = g.vector, g.tensor
-
-    g.sync.dma_start(T.xw[:, 0:F], T.x[:]).then_inc(sem.ldx, 16)
+    g.sync.dma_start(T.xd[:], T.x[:]).then_inc(sem.ldd, 16)
+    g.sync.dma_start(T.xs[:], T.x[:]).then_inc(sem.ldx, 16)
     if lead:
-        g.scalar.dma_start(T.xw[:, F:F + K], T.w[:]).then_inc(sem.ldw, 16)
+        sc.dma_start(T.wd[:], T.w[:]).then_inc(sem.ldwd, 16)
+        sc.dma_start(T.wo[:], T.w[:]).then_inc(sem.ldw, 16)
 
-    width = F + K if lead else F
     rid, pid, _ = topo.addr(cores[partner])
     m1 = topo.mask(core, cores[partner])
-    g.wait_ge(sem.ldx, 16)
-    if lead:
-        g.wait_ge(sem.ldw, 16)
-    g.remote_dma(out_ap=T.pw[:, 0:width], in_ap=T.xw[:, 0:width], remote_sem=sem.xarr, local_sem=sem.sent,
+    g.wait_ge(sem.ldd, 16)
+    g.remote_dma(out_ap=T.xp[:], in_ap=T.xd[:], remote_sem=sem.xarr, local_sem=sem.sent,
                  pid=pid, routing_id=rid, dma_engine_mask=m1)
     n_in = _engines(topo.mask(cores[partner], core))
+    left = _engines(m1)
 
-    v.memset(T.zero[:], 0.0).then_inc(sem.zs, 1)
-    v.wait_ge(sem.zs, 1)
+    if lead:
+        hs = [h for h, _ in plan[gi]]
+        mw = w_mask(core, hs[0])
+        g.wait_ge(sem.ldwd, 16)
+        g.remote_dma_fused([RemoteDMATransfer(dst_ids=ids_of(hs), dma_engine_mask=mw, remote_sem=sem.wharr,
+                                              srcs=[T.wd[:]], dsts=[T.whd[:] for _ in hs], alu_op=0)],
+                           local_sem=sem.sent)
+        left += _engines(mw)
+
+    v.memset(T.ones[:], 1.0).then_inc(sem.fill, 1)
+    g.wait_ge(sem.fill, 1)
+    g.affine_select(T.ident[:], T.ones[:], [[-1, 128]], AluOpType.is_equal, 0.0, 0, 1).then_inc(sem.ids, 1)
     v.wait_ge(sem.ldx, 16)
-    v.tensor_tensor(T.nx[:, 0:F], T.zero[:], T.xw[:, 0:F], AluOpType.subtract).then_inc(sem.ns, 1)
-    v.wait_ge(sem.ns, 1)
-
+    v.tensor_copy(T.xf[:, 0:F - N0], T.xs[:, N0:F]).then_inc(sem.cs, 1)
+    v.wait_ge(sem.cs, 1)
+    pe.wait_ge(sem.ids, 1)
     pe.wait_ge(sem.ldx, 16)
+    pe.matmul(T.sf[:, 0:N0], T.ident[:], T.xs[:, 0:N0], start=True, stop=False)
+
+    pe.wait_ge(sem.xarr, n_in)
+    pe.matmul(T.sf[:, 0:N0], T.ident[:], T.xp[:, 0:N0], start=False, stop=True).then_inc(sem.ps, 1)
+    sc.wait_ge(sem.ps, 1)
+    sc.activation(T.t[:, 0:N0], T.sf[:, 0:N0], relu).then_inc(sem.ts, 1)
+    v.wait_ge(sem.xarr, n_in)
+    v.tensor_tensor(T.s[:, N0:F], T.xf[:, 0:F - N0], T.xp[:, N0:F], AluOpType.add).then_inc(sem.as0, 1)
+    v.wait_ge(sem.as0, 1)
+    v.tensor_scalar(T.t[:, N0:F], T.s[:, N0:F], 0.0, None, AluOpType.max).then_inc(sem.ts, 1)
+
+    m2 = out_mask(core, dests)
+    g.wait_ge(sem.ts, 2)
+    g.remote_dma_fused([RemoteDMATransfer(dst_ids=ids_of([cores[d] for d in dests]), dma_engine_mask=m2,
+                                          remote_sem=sem["arr%d" % gi], srcs=[T.t[:]],
+                                          dsts=[T["tl%d" % gi][:] for _ in dests], alu_op=0)],
+                       local_sem=sem.sent)
+    left += _engines(m2)
+
+    pe.wait_ge(sem.ts, 2)
     if lead:
         pe.wait_ge(sem.ldw, 16)
-        wmat = T.xw[:, F:F + K]
+        wmat = T.wo[:]
     else:
-        pe.wait_ge(sem.xarr, n_in)
-        wmat = T.pw[:, F:F + K]
+        pe.wait_ge(sem["warr%d" % gi], w_engines(gi, rank))
+        wmat = T["wl%d" % gi][:]
     for c, (lo, hi) in enumerate(blocks):
-        pe.matmul(T["pf%d" % c][:, 0:H], wmat, T.xw[:, lo:hi], start=True, stop=False)
-
-    v.wait_ge(sem.xarr, n_in)
-    for c, (lo, hi) in enumerate(blocks):
-        v.tensor_tensor(T.m[:, lo:hi], T.nx[:, lo:hi], T.pw[:, lo:hi], AluOpType.max).then_inc(sem["ts%d" % c], 1)
-    for c, (lo, hi) in enumerate(blocks):
-        pe.wait_ge(sem["ts%d" % c], 1)
-        pe.matmul(T["pf%d" % c][:, 0:H], wmat, T.m[:, lo:hi], start=False, stop=True).then_inc(sem["ms%d" % c], 1)
-    for c, (lo, hi) in enumerate(blocks):
-        v.wait_ge(sem["ms%d" % c], 1)
-        v.tensor_copy(T.p[:, lo:hi], T["pf%d" % c][:, 0:H]).then_inc(sem.ps, 1)
-
-    m2 = topo.mask(core, cores[dests[0]])
-    ids = []
-    for d in dests:
-        m2 &= topo.mask(core, cores[d])
-        r, q, _ = topo.addr(cores[d])
-        ids.append(DstId(rid=r, pnc=q))
-    g.wait_ge(sem.ps, NH)
-    g.remote_dma_fused([RemoteDMATransfer(dst_ids=ids, dma_engine_mask=m2, remote_sem=sem["arr%d" % gi],
-                                          srcs=[T.p[:]], dsts=[T["land%d" % gi][:] for _ in dests], alu_op=0)],
-                       local_sem=sem.sent)
+        pe.matmul(T["yf%d" % c][:, 0:B], wmat, T.t[:, lo:hi], start=True, stop=False)
+    for i, (s, k) in enumerate(sources):
+        last = i == len(sources) - 1
+        pe.wait_ge(sem["warr%d" % k], w_engines(k, rank))
+        pe.wait_ge(sem["arr%d" % k], _engines(topo.mask(cores[s], core)))
+        for c, (lo, hi) in enumerate(blocks):
+            mm = pe.matmul(T["yf%d" % c][:, 0:B], T["wl%d" % k][:], T["tl%d" % k][:, lo:hi], start=False, stop=last)
+            if last:
+                mm.then_inc(sem["ms%d" % c], 1)
 
     for c, (lo, hi) in enumerate(blocks):
-        v.tensor_copy(T.af[:, lo:hi], T["pf%d" % c][:, 0:H]).then_inc(sem.gs, 1)
-    v.wait_ge(sem.gs, NH)
-
-    (s1, k1), (s2, k2) = sources
-    v.wait_ge(sem["arr%d" % k1], _engines(topo.mask(cores[s1], core)))
-    v.tensor_tensor(T.af[:, F:2 * F], T.af[:, 0:F], T["land%d" % k1][:], AluOpType.add).then_inc(sem.as1, 1)
-    v.wait_ge(sem.as1, 1)
-    v.wait_ge(sem["arr%d" % k2], _engines(topo.mask(cores[s2], core)))
-    v.tensor_tensor(T.ysb[:], T.af[:, F:2 * F], T["land%d" % k2][:], AluOpType.add).then_inc(sem.ys, 1)
-    g.sync.wait_ge(sem.ys, 1)
+        if c % 2 == 0:
+            v.wait_ge(sem["ms%d" % c], 1)
+            v.tensor_copy(T.ysb[:, lo:hi], T["yf%d" % c][:, 0:B]).then_inc(sem.ys, 1)
+        else:
+            sc.wait_ge(sem["ms%d" % c], 1)
+            sc.activation(T.ysb[:, lo:hi], T["yf%d" % c][:, 0:B], copy).then_inc(sem.ys, 1)
+    g.sync.wait_ge(sem.ys, NB)
     g.sync.dma_start(T.y[:], T.ysb[:]).then_inc(sem.st, 16)
     g.sync.wait_ge(sem.st, 16)
 
-    g.wait_ge(sem.sent, _engines(m1) + _engines(m2))
+    g.wait_ge(sem.sent, left)

from concourse.bass import DstId, RemoteDMATransfer
from concourse.mybir import AluOpType, ActivationFunctionType

F = 256
K = 128
N0 = 112
NB = 4
B = F // NB

SCRATCH = {
    "xd": ("dram", [128, F], "bfloat16"),
    "xs": ("sbuf", [128, F], "bfloat16"),
    "xp": ("sbuf", [128, F], "bfloat16"),
    "wd": ("dram", [128, K], "bfloat16"),
    "wo": ("sbuf", [128, K], "bfloat16"),
    "whd": ("dram", [128, K], "bfloat16"),
    "ones": ("sbuf", [128, 128], "bfloat16"),
    "ident": ("sbuf", [128, 128], "bfloat16"),
    "s": ("sbuf", [128, F], "bfloat16"),
    "t": ("sbuf", [128, F], "bfloat16"),
    "ysb": ("sbuf", [128, F], "bfloat16"),
    "xf": ("psum", [128, 512], "float32"),
    "sf": ("psum", [128, 512], "float32"),
}
for _k in range(3):
    SCRATCH["wl%d" % _k] = ("sbuf", [128, K], "bfloat16")
    SCRATCH["tl%d" % _k] = ("sbuf", [128, F], "bfloat16")
for _c in range(NB):
    SCRATCH["yf%d" % _c] = ("psum", [128, 512], "float32")
SEMAPHORES = (["ldd", "ldx", "ldwd", "ldw", "xarr", "sent", "cs", "fill", "ids", "ps", "as0", "ts", "ys", "st",
               "wharr"]
              + ["%s%d" % (s, k) for s in ("warr", "arr") for k in range(3)]
              + ["ms%d" % c for c in range(NB)])


def _engines(mask):
    return bin(mask).count("1")


def _every_other(mask):
    bits = [i for i in range(mask.bit_length()) if (mask >> i) & 1]
    return sum(1 << i for i in bits[::2])


def _forwarders(T, topo, groups):
    cores = T.cores
    plan = {}
    for k, members in enumerate(groups):
        lead = cores[members[0]]
        idle = [c for c in range(topo.CHIPS * topo.CORES_PER_CHIP)
                if topo.chip(c) == topo.chip(lead) and topo.die(c) != topo.die(lead) and T.rank_of(c) is None]
        others = [d for d in range(len(cores)) if d != members[0]]
        near = [d for d in others if topo.same_plane(topo.chip(lead), topo.chip(cores[d]))]
        far = [d for d in others if d not in near]
        owners = [c for c in idle if all(topo.may_write(c, cores[d]) for d in far)]
        rest = [c for c in idle if c not in owners and all(topo.may_write(c, cores[d]) for d in near)]
        half = (len(far) + 1) // 2
        plan[k] = [(owners[0], far[:half]), (owners[1], far[half:]), (rest[0], near)]
    return plan


def rank_program(g, core, T, topo):
    groups = T.tables["GROUPS"]
    cores = T.cores
    n = len(cores)
    sem = T.sem
    plan = _forwarders(T, topo, groups)
    rank = T.rank_of(core)

    def w_mask(lead_core, helper):
        off = [c for c in cores if topo.chip(c) != topo.chip(lead_core)][0]
        m = topo.mask(lead_core, helper) & ~topo.mask(lead_core, off)
        return _every_other(m if m else topo.mask(lead_core, helper))

    def out_mask(src, served):
        mk = topo.mask(src, cores[served[0]])
        for d in served:
            mk &= topo.mask(src, cores[d])
        return mk

    def ids_of(cs):
        out = []
        for c in cs:
            r, q, _ = topo.addr(c)
            out.append(DstId(rid=r, pnc=q))
        return out

    if rank is None:
        for k in plan:
            for h, served in plan[k]:
                if h != core:
                    continue
                mk = out_mask(core, served)
                g.wait_ge(sem.wharr, _engines(w_mask(cores[groups[k][0]], core)))
                g.remote_dma_fused([RemoteDMATransfer(dst_ids=ids_of([cores[d] for d in served]), dma_engine_mask=mk,
                                                      remote_sem=sem["warr%d" % k], srcs=[T.whd[:]],
                                                      dsts=[T["wl%d" % k][:] for _ in served], alu_op=0)],
                                   local_sem=sem.sent)
                g.wait_ge(sem.sent, _engines(mk))
        return

    gi = [k for k, m in enumerate(groups) if rank in m][0]
    members = groups[gi]
    lead = members[0] == rank
    partner = [m for m in members if m != rank][0]

    def sender_of(k, d):
        for near in (topo.same_plane, topo.mates):
            for m in groups[k]:
                if near(topo.chip(cores[m]), topo.chip(cores[d])) and topo.may_write(cores[m], cores[d]):
                    return m
        return [m for m in groups[k] if topo.may_write(cores[m], cores[d])][0]

    def w_engines(k, d):
        for h, served in plan[k]:
            if d in served:
                return _engines(out_mask(h, served))

    dests = sorted([d for d in range(n) if d not in members and sender_of(gi, d) == rank],
                   key=lambda d: (d - rank) % n)
    sources = sorted([(sender_of(k, rank), k) for k in range(len(groups)) if k != gi],
                     key=lambda s: (rank - s[0]) % n)
    blocks = [(c * B, (c + 1) * B) for c in range(NB)]
    v, pe, sc = g.vector, g.tensor, g.scalar
    relu, copy = ActivationFunctionType.Relu, ActivationFunctionType.Copy

    g.sync.dma_start(T.xd[:], T.x[:]).then_inc(sem.ldd, 16)
    g.sync.dma_start(T.xs[:], T.x[:]).then_inc(sem.ldx, 16)
    if lead:
        sc.dma_start(T.wd[:], T.w[:]).then_inc(sem.ldwd, 16)
        sc.dma_start(T.wo[:], T.w[:]).then_inc(sem.ldw, 16)

    rid, pid, _ = topo.addr(cores[partner])
    m1 = topo.mask(core, cores[partner])
    g.wait_ge(sem.ldd, 16)
    g.remote_dma(out_ap=T.xp[:], in_ap=T.xd[:], remote_sem=sem.xarr, local_sem=sem.sent,
                 pid=pid, routing_id=rid, dma_engine_mask=m1)
    n_in = _engines(topo.mask(cores[partner], core))
    left = _engines(m1)

    if lead:
        hs = [h for h, _ in plan[gi]]
        mw = w_mask(core, hs[0])
        g.wait_ge(sem.ldwd, 16)
        g.remote_dma_fused([RemoteDMATransfer(dst_ids=ids_of(hs), dma_engine_mask=mw, remote_sem=sem.wharr,
                                              srcs=[T.wd[:]], dsts=[T.whd[:] for _ in hs], alu_op=0)],
                           local_sem=sem.sent)
        left += _engines(mw)

    v.memset(T.ones[:], 1.0).then_inc(sem.fill, 1)
    g.wait_ge(sem.fill, 1)
    g.affine_select(T.ident[:], T.ones[:], [[-1, 128]], AluOpType.is_equal, 0.0, 0, 1).then_inc(sem.ids, 1)
    v.wait_ge(sem.ldx, 16)
    v.tensor_copy(T.xf[:, 0:F - N0], T.xs[:, N0:F]).then_inc(sem.cs, 1)
    v.wait_ge(sem.cs, 1)
    pe.wait_ge(sem.ids, 1)
    pe.wait_ge(sem.ldx, 16)
    pe.matmul(T.sf[:, 0:N0], T.ident[:], T.xs[:, 0:N0], start=True, stop=False)

    pe.wait_ge(sem.xarr, n_in)
    pe.matmul(T.sf[:, 0:N0], T.ident[:], T.xp[:, 0:N0], start=False, stop=True).then_inc(sem.ps, 1)
    sc.wait_ge(sem.ps, 1)
    sc.activation(T.t[:, 0:N0], T.sf[:, 0:N0], relu).then_inc(sem.ts, 1)
    v.wait_ge(sem.xarr, n_in)
    v.tensor_tensor(T.s[:, N0:F], T.xf[:, 0:F - N0], T.xp[:, N0:F], AluOpType.add).then_inc(sem.as0, 1)
    v.wait_ge(sem.as0, 1)
    v.tensor_scalar(T.t[:, N0:F], T.s[:, N0:F], 0.0, None, AluOpType.max).then_inc(sem.ts, 1)

    m2 = out_mask(core, dests)
    g.wait_ge(sem.ts, 2)
    g.remote_dma_fused([RemoteDMATransfer(dst_ids=ids_of([cores[d] for d in dests]), dma_engine_mask=m2,
                                          remote_sem=sem["arr%d" % gi], srcs=[T.t[:]],
                                          dsts=[T["tl%d" % gi][:] for _ in dests], alu_op=0)],
                       local_sem=sem.sent)
    left += _engines(m2)

    pe.wait_ge(sem.ts, 2)
    if lead:
        pe.wait_ge(sem.ldw, 16)
        wmat = T.wo[:]
    else:
        pe.wait_ge(sem["warr%d" % gi], w_engines(gi, rank))
        wmat = T["wl%d" % gi][:]
    for c, (lo, hi) in enumerate(blocks):
        pe.matmul(T["yf%d" % c][:, 0:B], wmat, T.t[:, lo:hi], start=True, stop=False)
    for i, (s, k) in enumerate(sources):
        last = i == len(sources) - 1
        pe.wait_ge(sem["warr%d" % k], w_engines(k, rank))
        pe.wait_ge(sem["arr%d" % k], _engines(topo.mask(cores[s], core)))
        for c, (lo, hi) in enumerate(blocks):
            mm = pe.matmul(T["yf%d" % c][:, 0:B], T["wl%d" % k][:], T["tl%d" % k][:, lo:hi], start=False, stop=last)
            if last:
                mm.then_inc(sem["ms%d" % c], 1)

    for c, (lo, hi) in enumerate(blocks):
        if c % 2 == 0:
            v.wait_ge(sem["ms%d" % c], 1)
            v.tensor_copy(T.ysb[:, lo:hi], T["yf%d" % c][:, 0:B]).then_inc(sem.ys, 1)
        else:
            sc.wait_ge(sem["ms%d" % c], 1)
            sc.activation(T.ysb[:, lo:hi], T["yf%d" % c][:, 0:B], copy).then_inc(sem.ys, 1)
    g.sync.wait_ge(sem.ys, NB)
    g.sync.dma_start(T.y[:], T.ysb[:]).then_inc(sem.st, 16)
    g.sync.wait_ge(sem.st, 16)

    g.wait_ge(sem.sent, left)
